import numpy as np
import ml_dtypes


def mxq(x, axis, fmt="e4m3"):
    dtype, down = {"e4m3": (ml_dtypes.float8_e4m3fn, 7), "e5m2": (ml_dtypes.float8_e5m2, 14)}[fmt]
    v = np.moveaxis(np.asarray(x, np.float32).astype(ml_dtypes.bfloat16).astype(np.float64), axis, -1)
    blocks = v.reshape(v.shape[:-1] + (-1, 32))
    amax = np.abs(blocks).max(-1, keepdims=True)
    byte = np.maximum(np.where(amax > 0, np.frexp(amax)[1] - 1 + 127, 0) - down, 1)
    scale = np.exp2(byte - 127.0)
    codes = (blocks / scale).astype(np.float32).astype(dtype).astype(np.float64)
    return np.moveaxis((codes * scale).reshape(v.shape), -1, axis)


WIDE = False


def mx_kscale(k):
    if not WIDE:
        return np.ones(k)
    levels = np.array([10, -10, 5, -5, 0])
    if k % 512:
        return np.exp2(np.random.permutation(np.resize(levels, k // 32))).repeat(32)
    a = np.empty((k // 512, 16))
    for p in range(k // 512):
        a[p, :8] = np.random.permutation(np.resize(levels, 8))
        for g in range(8):
            far = levels[np.abs(levels - a[p, g]) >= 10]
            a[p, g + 8] = far[np.random.randint(len(far))]
    return np.exp2(a.ravel()).repeat(32)


def f64(x):
    return np.asarray(x).astype(np.float64)


def striped(idx):
    return np.tile(np.asarray(idx).reshape(-1, 16).T, (8, 1)).astype(np.uint16)


def unstriped(offs):
    return offs[:16].T.reshape(-1).astype(np.int64)


E2M1 = np.array([0.0, 0.5, 1.0, 1.5, 2.0, 3.0, 4.0, 6.0, -0.0, -0.5, -1.0, -1.5, -2.0, -3.0, -4.0, -6.0])


def pack_weight(w, fmt):
    k, n = w.shape
    w = f64(np.asarray(w, np.float32).astype(ml_dtypes.bfloat16)).reshape(k // 32, 32, n)
    amax = np.abs(w).max(1)
    if fmt == "e4m3":
        byte = np.frexp(amax)[1] - 1 + 127 - 7
    else:
        mant, ex = np.frexp(amax / 6.0)
        byte = np.where(mant > 0.5, ex, ex - 1) + 127
    byte = np.clip(np.where(amax > 0, byte, 1), 1, 254)
    scaled = (w * np.exp2(127.0 - byte)[:, None, :]).reshape(k, n).astype(np.float32)
    by_word = np.ascontiguousarray(scaled.reshape(k // 512, 128, 4, n).transpose(0, 1, 3, 2))
    if fmt == "e4m3":
        words = by_word.astype(ml_dtypes.float8_e4m3fn).view(np.uint8)
    else:
        c = by_word.astype(ml_dtypes.float4_e2m1fn).view(np.uint8) & 0xF
        words = (c[..., 0::2] | (c[..., 1::2] << 4)).reshape(k // 512, 128, 2 * n)
    return np.ascontiguousarray(words), np.ascontiguousarray(byte.astype(np.uint8).reshape(k // 512, 16, n))


def unpack_weight(words, scales, fmt):
    g, _, n = scales.shape
    words = np.ascontiguousarray(words).reshape(g, 128, n, -1)
    if fmt == "e4m3":
        vals = words.view(ml_dtypes.float8_e4m3fn).astype(np.float64)
    else:
        nib = np.empty((g, 128, n, 4), np.uint8)
        nib[..., 0::2] = words & 0xF
        nib[..., 1::2] = words >> 4
        vals = E2M1[nib]
    vals = vals * np.repeat(np.exp2(scales.astype(np.float64) - 127.0), 8, axis=1)[..., None]
    return vals.transpose(0, 1, 3, 2).reshape(g * 512, n)


def sigmoid(v):
    return 1.0 / (1.0 + np.exp(-v))


D, E, T, I, Q, G = 512, 512, 1024, 256, 512, 32


def setup_inputs():
    n = np.random.standard_normal
    idx = np.random.permutation(T)[:I]
    fd = mx_kscale(D)
    fq = mx_kscale(Q)
    keysp = pack_weight(n((D, T)) / fd[:, None], "e2m1")
    return {
        "query": (n((D, Q)) * 0.6 / np.sqrt(D) * fd[:, None]).astype(np.float32),
        "keys_words": keysp[0],
        "keys_scales": keysp[1],
        "size": (np.random.uniform(0.5, 2.0, (1, I))).astype(np.float32),
        "qs": (np.random.uniform(2.0, 8.0, (Q, 1)) * fq[:, None]).astype(np.float32),
        "grows": (n((Q, E)) / fq[:, None]).astype(np.float32),
        "old": (n((E, T)) * 2.0).astype(np.float32),
        "fade": (np.random.uniform(0.5, 1.0, (1, T))).astype(np.float32),
        "offs": striped(idx),
    }


def reference(query, keys_words, keys_scales, size, qs, grows, old, fade, offs):
    idx = unstriped(offs)
    keysu = unpack_weight(keys_words, keys_scales, "e2m1")
    queryq = mxq(f64(query), 0, "e4m3")
    keysidxg = keysu[:, idx]
    a = queryq.T @ keysidxg
    s = a.reshape(Q, G, I // G).mean(axis=2)
    p = np.exp(s - np.max(s, axis=1, keepdims=True))
    z = np.sum(p, axis=1, keepdims=True)
    r = p / z
    rr = np.repeat(r, I // G, axis=1)
    w = rr * sigmoid(a) * f64(size)
    wq = w * f64(qs)
    growsq = mxq(f64(grows), 0, "e4m3")
    wqq = mxq(wq, 0, "e4m3")
    gv = growsq.T @ wqq
    gf = np.zeros((E, T))
    gf[:, idx] = gv
    y = f64(old) * f64(fade) + gf
    return y

@@ -1,0 +1,243 @@
+from contextlib import ExitStack
+
+import concourse.mybir as mybir
+from concourse.masks import make_identity
+
+D, E, T, I, Q, G = 512, 512, 1024, 256, 512, 32
+FLOPS = 2 * D * Q * I + 2 * Q * E * I
+
+F32 = mybir.dt.float32
+BF16 = mybir.dt.bfloat16
+I32 = mybir.dt.int32
+U32 = mybir.dt.uint32
+U16 = mybir.dt.uint16
+U8 = mybir.dt.uint8
+FP8X4 = mybir.dt.float8_e4m3fn_x4
+FP4X4 = mybir.dt.float4_e2m1fn_x4
+ALU = mybir.AluOpType
+ACT = mybir.ActivationFunctionType
+AXIS_X = mybir.AxisListType.X
+
+P = 128
+PACK = 4
+SPAN = I // G
+E_TILES = E // P
+T_CHUNKS = T // P
+BANK = 512
+GPSIMD_TILES = 2
+
+
+def tile_attend_bspanread_v_kernel(tc, query, keys_words, keys_scales, size, qs, grows, old, fade, offs, out):
+    nc = tc.nc
+    with ExitStack() as ctx:
+        keep = ctx.enter_context(tc.tile_pool(name="keep", bufs=1))
+        ps_mm = ctx.enter_context(tc.psum_pool(name="ps_mm", bufs=2))
+        ps_vec = ctx.enter_context(tc.psum_pool(name="ps_vec", bufs=1))
+        ps_turn = ctx.enter_context(tc.psum_pool(name="ps_turn", bufs=2))
+        ps_back = ctx.enter_context(tc.psum_pool(name="ps_back", bufs=3))
+
+        offsets = keep.tile([P, I // 16], U16, name="offsets")
+        nc.sync.dma_start(offsets[:], offs)
+        pool_scales = keep.tile([P, T], U8, name="pool_scales", tag="then_old0", align_bytes=64)
+        nc.vector.memset(pool_scales[:].bitcast(I32), 0)
+        rows = keep.tile([P, P], F32, name="rows")
+        nc.gpsimd.memset(rows[:], 0.0)
+        pool_words = keep.tile([P, T], U16, name="pool_words", tag="then_grows")
+        nc.sync.dma_start(pool_words[:].bitcast(I32), keys_words[0].bitcast(I32))
+        for quad in range(4):
+            nc.scalar.dma_start(
+                pool_scales[32 * quad : 32 * quad + 4, :].bitcast(I32),
+                keys_scales[0, 4 * quad : 4 * quad + 4, :].bitcast(I32),
+            )
+        query_rows = query.rearrange("(p j) q -> p j q", j=PACK)
+        query_raw = []
+        for half in range(2):
+            raw = keep.tile([P, PACK, Q // 2], F32, name=f"query_raw{half}", tag=f"then_old{half + 1}", align_bytes=64)
+            nc.sync.dma_start(raw[:], query_rows[:, :, half * (Q // 2) : (half + 1) * (Q // 2)])
+            query_raw.append(raw)
+        qs_cols = keep.tile([P, PACK], F32, name="qs_cols")
+        nc.gpsimd.dma_start(rows[T_CHUNKS : T_CHUNKS + 2, :], size.rearrange("one (c p) -> (one c) p", p=P))
+        nc.gpsimd.dma_start(rows[0:T_CHUNKS, :], fade.rearrange("one (c p) -> (one c) p", p=P))
+        nc.gpsimd.dma_start(qs_cols[:], qs.rearrange("(s r) one -> s (r one)", r=PACK))
+        ident = keep.tile([P, P], F32, name="ident")
+        make_identity(nc, ident[:])
+
+        key_words = keep.tile([P, I], U16, name="key_words", align_bytes=64)
+        key_scales = keep.tile([P, I], U8, name="key_scales", align_bytes=64)
+        nc.vector.tensor_copy(key_words[:], pool_words[:].indirect(offsets[:]))
+        nc.vector.tensor_copy(key_scales[:], pool_scales[:].indirect(offsets[:]))
+
+        query_codes = [keep.tile([P, P], U32, name=f"query_codes{r}", align_bytes=64) for r in range(PACK)]
+        query_scales = [keep.tile([P, P], U8, name=f"query_scales{r}", align_bytes=64) for r in range(PACK)]
+        for half in range(2):
+            dealt = keep.tile([P, PACK, P // 2, PACK], BF16, name=f"query_dealt{half}", tag=("then_old3", "dealt1")[half], align_bytes=64)
+            nc.vector.tensor_copy(
+                dealt[:].rearrange("p r s j -> p s r j"),
+                query_raw[half][:].rearrange("p j (s r) -> p s r j", r=PACK),
+            )
+            cols = slice(half * (P // 2), (half + 1) * (P // 2))
+            for r in range(PACK):
+                nc.vector.quantize_mx(
+                    out=query_codes[r][:, cols].bitcast(FP8X4),
+                    scales=query_scales[r][:, cols],
+                    in_=dealt[:, r].rearrange("p s j -> p (s j)"),
+                )
+
+        grows_raw = keep.tile([P, PACK, E], F32, name="grows_raw", tag="then_grows")
+        nc.sync.dma_start(grows_raw[:], grows.rearrange("(s r) e -> s r e", r=PACK))
+        old_tiles = []
+        for j in range(E_TILES):
+            old_tile = keep.tile([P, T], F32, name=f"old{j}", tag=f"then_old{j}", align_bytes=64)
+            nc.sync.dma_start(old_tile[:], old[j * P : (j + 1) * P, :])
+            old_tiles.append(old_tile)
+
+        vec_bank = ps_vec.tile([P, P + I], F32, name="vec_bank")
+        nc.tensor.transpose(vec_bank[:, 0:P], rows[:], ident[:])
+        vec_cols = keep.tile([P, 16], F32, name="vec_cols")
+        nc.scalar.copy(vec_cols[:], vec_bank[:, 0:16])
+        for half in range(2):
+            col = T_CHUNKS + half
+            nc.tensor.transpose(
+                vec_bank[:, P + half * P : P + (half + 1) * P],
+                vec_cols[:, col : col + 1].to_broadcast([P, P]),
+                ident[:],
+            )
+
+        score_banks = []
+        for half in range(2):
+            score_banks.append(ps_mm.tile([P, PACK, P], F32, name=f"scores{half}", tag="mm"))
+        for r in range(PACK):
+            for half in range(2):
+                slots = slice(half * P, (half + 1) * P)
+                nc.tensor.matmul_mx(
+                    out=score_banks[half][:, r, :],
+                    lhsT=query_codes[r][:].bitcast(FP8X4),
+                    lhsT_scale=query_scales[r][:],
+                    rhs=key_words[:, slots].bitcast(FP4X4),
+                    rhs_scale=key_scales[:, slots],
+                    start=True,
+                    stop=True,
+                )
+
+        span_sums = keep.tile([P, PACK, G], F32, name="span_sums")
+        gates = [keep.tile([P, P, PACK], F32, name=f"gates{half}") for half in range(2)]
+        for half in range(2):
+            nc.vector.tensor_reduce(
+                out=span_sums[:, :, half * (G // 2) : (half + 1) * (G // 2)],
+                in_=score_banks[half][:].rearrange("p r (g m) -> p r g m", m=SPAN),
+                axis=AXIS_X,
+                op=ALU.add,
+            )
+            other = 1 - half
+            nc.scalar.activation(gates[other][:], score_banks[other][:].rearrange("p r i -> p i r"), ACT.Sigmoid)
+
+        neg_max = keep.tile([P, PACK], F32, name="neg_max")
+        nc.vector.tensor_reduce(out=neg_max[:], in_=span_sums[:], axis=AXIS_X, op=ALU.max, negate=True)
+        shifted = keep.tile([P, PACK, G], F32, name="shifted", tag="after_exp", align_bytes=64)
+        nc.vector.tensor_tensor(shifted[:], span_sums[:], neg_max[:].unsqueeze(2).to_broadcast([P, PACK, G]), ALU.add)
+        probs = keep.tile([P, PACK, G], F32, name="probs")
+        nc.scalar.activation(probs[:], shifted[:], ACT.Exp, scale=1.0 / SPAN)
+        row_sums = keep.tile([P, PACK], F32, name="row_sums")
+        nc.vector.tensor_reduce(out=row_sums[:], in_=probs[:], axis=AXIS_X, op=ALU.add)
+        probs_qs = keep.tile([P, PACK, G], F32, name="probs_qs")
+        nc.vector.tensor_tensor(probs_qs[:], probs[:], qs_cols[:].unsqueeze(2).to_broadcast([P, PACK, G]), ALU.mult)
+        inv_sums = keep.tile([P, PACK], F32, name="inv_sums")
+        nc.vector.reciprocal(inv_sums[:], row_sums[:])
+        shares = keep.tile([P, G, PACK], F32, name="shares")
+        nc.vector.tensor_tensor(
+            shares[:],
+            probs_qs[:].rearrange("p r g -> p g r"),
+            inv_sums[:].unsqueeze(1).to_broadcast([P, G, PACK]),
+            ALU.mult,
+        )
+
+        sized = [keep.tile([P, P, PACK], F32, name=f"sized{half}") for half in (0, 1)]
+        for half in (1, 0):
+            nc.vector.tensor_tensor(
+                sized[half][:],
+                gates[half][:],
+                vec_bank[:, P + half * P : P + (half + 1) * P].unsqueeze(2).to_broadcast([P, P, PACK]),
+                ALU.mult,
+            )
+        weights = [keep.tile([P, G // 2, SPAN, PACK], BF16, name=f"weights{half}", align_bytes=64) for half in (0, 1)]
+        for half in range(2):
+            nc.vector.tensor_tensor(
+                weights[half][:],
+                sized[half][:].rearrange("p (g m) r -> p g m r", m=SPAN),
+                shares[:, half * (G // 2) : (half + 1) * (G // 2), :].unsqueeze(2).to_broadcast([P, G // 2, SPAN, PACK]),
+                ALU.mult,
+            )
+        weight_codes = keep.tile([P, I], U32, name="weight_codes", align_bytes=64)
+        weight_scales = keep.tile([P, I], U8, name="weight_scales", align_bytes=64)
+        for half in range(2):
+            slots = slice(half * P, (half + 1) * P)
+            nc.vector.quantize_mx(
+                out=weight_codes[:, slots].bitcast(FP8X4),
+                scales=weight_scales[:, slots],
+                in_=weights[half][:].rearrange("p g m r -> p (g m r)"),
+            )
+
+        grows_lo = keep.tile([P, E // 2, PACK], BF16, name="grows_lo", align_bytes=64)
+        grows_hi = keep.tile([P, E // 2, PACK], BF16, name="grows_hi", tag="after_exp", align_bytes=64)
+        for j in range(2):
+            nc.vector.tensor_copy(
+                grows_lo[:, j * P : (j + 1) * P, :].rearrange("p (c i) r -> p c r i", i=4),
+                grows_raw[:, :, j * P : (j + 1) * P].rearrange("p r (c i) -> p c r i", i=4),
+            )
+        nc.scalar.copy(
+            grows_hi[:].rearrange("p (c i) r -> p c r i", i=4),
+            grows_raw[:, :, E // 2 : E].rearrange("p r (c i) -> p c r i", i=4),
+        )
+        grows_codes = [keep.tile([P, P], U32, name=f"grows_codes{j}", align_bytes=64) for j in range(E_TILES)]
+        grows_scales = [keep.tile([P, P], U8, name=f"grows_scales{j}", align_bytes=64) for j in range(E_TILES)]
+        for j in range(E_TILES):
+            woven = grows_lo if j < 2 else grows_hi
+            nc.vector.quantize_mx(
+                out=grows_codes[j][:].bitcast(FP8X4),
+                scales=grows_scales[j][:],
+                in_=woven[:, (j % 2) * P : (j % 2 + 1) * P, :].rearrange("p e r -> p (e r)"),
+            )
+
+        placed = []
+        for j in range(E_TILES):
+            window = keep.tile([P, T], F32, name=f"placed{j}")
+            nc.vector.memset(window[:].bitcast(I32), 0)
+            bank = ps_mm.tile([P, I], F32, name=f"grad_bank{j}", tag="mm")
+            nc.tensor.matmul_mx(
+                out=bank[:],
+                lhsT=grows_codes[j][:].bitcast(FP8X4),
+                lhsT_scale=grows_scales[j][:],
+                rhs=weight_codes[:].bitcast(FP8X4),
+                rhs_scale=weight_scales[:],
+                start=True,
+                stop=True,
+            )
+            grads = keep.tile([P, I], F32, name=f"grads{j}")
+            nc.scalar.copy(grads[:], bank[:])
+            nc.vector.tensor_copy(window[:].indirect(offsets[:]), grads[:])
+            placed.append(window)
+
+        per_bank = BANK // P
+        for j in range(E_TILES):
+            faded_t = keep.tile([P, T_CHUNKS, P], F32, name=f"faded_t{j}")
+            for b in range(T // BANK):
+                turned = ps_turn.tile([P, per_bank, P], F32, name="turned")
+                for k in range(per_bank):
+                    c = b * per_bank + k
+                    nc.tensor.transpose(turned[:, k, :], old_tiles[j][:, c * P : (c + 1) * P], ident[:])
+                for k in range(per_bank):
+                    c = b * per_bank + k
+                    nc.scalar.activation(faded_t[:, c, :], turned[:, k, :], ACT.Copy, scale=vec_cols[:, c : c + 1])
+            for b in range(T // BANK):
+                cols = slice(b * BANK, (b + 1) * BANK)
+                back = ps_back.tile([P, BANK], F32, name="back")
+                for k in range(per_bank):
+                    nc.tensor.transpose(back[:, k * P : (k + 1) * P], faded_t[:, b * per_bank + k, :], ident[:])
+                result = keep.tile([P, BANK], F32, name=f"result{j}_{b}")
+                if j < GPSIMD_TILES:
+                    faded = keep.tile([P, BANK], F32, name=f"faded{j}_{b}")
+                    nc.scalar.copy(faded[:], back[:])
+                    nc.gpsimd.tensor_tensor(result[:], faded[:], placed[j][:, cols], ALU.add)
+                else:
+                    nc.vector.tensor_tensor(result[:], back[:], placed[j][:, cols], ALU.add)
+                nc.sync.dma_start(out[j * P : (j + 1) * P, cols], result[:])

@@ -39,7 +39,7 @@ def tile_attend_bspanread_v_kernel(tc, query, keys_words, keys_scales, size, qs,
         offsets = keep.tile([P, I // 16], U16, name="offsets")
         nc.sync.dma_start(offsets[:], offs)
         pool_scales = keep.tile([P, T], U8, name="pool_scales", tag="then_old0", align_bytes=64)
-        nc.vector.memset(pool_scales[:].bitcast(I32), 0)
+        nc.gpsimd.memset(pool_scales[:].bitcast(I32), 0)
         rows = keep.tile([P, P], F32, name="rows")
         nc.gpsimd.memset(rows[:], 0.0)
         pool_words = keep.tile([P, T], U16, name="pool_words", tag="then_grows")
@@ -56,9 +56,12 @@ def tile_attend_bspanread_v_kernel(tc, query, keys_words, keys_scales, size, qs,
             nc.sync.dma_start(raw[:], query_rows[:, :, half * (Q // 2) : (half + 1) * (Q // 2)])
             query_raw.append(raw)
         qs_cols = keep.tile([P, PACK], F32, name="qs_cols")
-        nc.gpsimd.dma_start(rows[T_CHUNKS : T_CHUNKS + 2, :], size.rearrange("one (c p) -> (one c) p", p=P))
-        nc.gpsimd.dma_start(rows[0:T_CHUNKS, :], fade.rearrange("one (c p) -> (one c) p", p=P))
-        nc.gpsimd.dma_start(qs_cols[:], qs.rearrange("(s r) one -> s (r one)", r=PACK))
+        nc.sync.dma_start(qs_cols[:], qs.rearrange("(s r) one -> s (r one)", r=PACK))
+        nc.sync.dma_start(rows[0:T_CHUNKS, :], fade.rearrange("one (c p) -> (one c) p", p=P))
+        size_cols = keep.tile([P, 2], F32, name="size_cols")
+        with nc.allow_non_contiguous_dma(reason="one value of size to a partition"):
+            nc.scalar.dma_start(size_cols[:], size.rearrange("one (h p) -> p (one h)", p=P))
+
         ident = keep.tile([P, P], F32, name="ident")
         make_identity(nc, ident[:])
 
@@ -92,22 +95,18 @@ def tile_attend_bspanread_v_kernel(tc, query, keys_words, keys_scales, size, qs,
             old_tiles.append(old_tile)
 
         vec_bank = ps_vec.tile([P, P + I], F32, name="vec_bank")
-        nc.tensor.transpose(vec_bank[:, 0:P], rows[:], ident[:])
-        vec_cols = keep.tile([P, 16], F32, name="vec_cols")
-        nc.scalar.copy(vec_cols[:], vec_bank[:, 0:16])
         for half in range(2):
-            col = T_CHUNKS + half
             nc.tensor.transpose(
                 vec_bank[:, P + half * P : P + (half + 1) * P],
-                vec_cols[:, col : col + 1].to_broadcast([P, P]),
+                size_cols[:, half : half + 1].to_broadcast([P, P]),
                 ident[:],
             )
 
         score_banks = []
         for half in range(2):
             score_banks.append(ps_mm.tile([P, PACK, P], F32, name=f"scores{half}", tag="mm"))
-        for r in range(PACK):
-            for half in range(2):
+        for half in range(2):
+            for r in range(PACK):
                 slots = slice(half * P, (half + 1) * P)
                 nc.tensor.matmul_mx(
                     out=score_banks[half][:, r, :],
@@ -122,24 +121,23 @@ def tile_attend_bspanread_v_kernel(tc, query, keys_words, keys_scales, size, qs,
         span_sums = keep.tile([P, PACK, G], F32, name="span_sums")
         gates = [keep.tile([P, P, PACK], F32, name=f"gates{half}") for half in range(2)]
         for half in range(2):
+            nc.scalar.activation(gates[half][:], score_banks[half][:].rearrange("p r i -> p i r"), ACT.Sigmoid)
             nc.vector.tensor_reduce(
                 out=span_sums[:, :, half * (G // 2) : (half + 1) * (G // 2)],
                 in_=score_banks[half][:].rearrange("p r (g m) -> p r g m", m=SPAN),
                 axis=AXIS_X,
                 op=ALU.add,
             )
-            other = 1 - half
-            nc.scalar.activation(gates[other][:], score_banks[other][:].rearrange("p r i -> p i r"), ACT.Sigmoid)
 
         neg_max = keep.tile([P, PACK], F32, name="neg_max")
         nc.vector.tensor_reduce(out=neg_max[:], in_=span_sums[:], axis=AXIS_X, op=ALU.max, negate=True)
         shifted = keep.tile([P, PACK, G], F32, name="shifted", tag="after_exp", align_bytes=64)
         nc.vector.tensor_tensor(shifted[:], span_sums[:], neg_max[:].unsqueeze(2).to_broadcast([P, PACK, G]), ALU.add)
-        probs = keep.tile([P, PACK, G], F32, name="probs")
+        probs = keep.tile([P, PACK, G], F32, name="probs", tag="after_exp2", align_bytes=64)
         nc.scalar.activation(probs[:], shifted[:], ACT.Exp, scale=1.0 / SPAN)
         row_sums = keep.tile([P, PACK], F32, name="row_sums")
         nc.vector.tensor_reduce(out=row_sums[:], in_=probs[:], axis=AXIS_X, op=ALU.add)
-        probs_qs = keep.tile([P, PACK, G], F32, name="probs_qs")
+        probs_qs = keep.tile([P, PACK, G], F32, name="probs_qs", tag="fade_row1", align_bytes=64)
         nc.vector.tensor_tensor(probs_qs[:], probs[:], qs_cols[:].unsqueeze(2).to_broadcast([P, PACK, G]), ALU.mult)
         inv_sums = keep.tile([P, PACK], F32, name="inv_sums")
         nc.vector.reciprocal(inv_sums[:], row_sums[:])
@@ -151,15 +149,15 @@ def tile_attend_bspanread_v_kernel(tc, query, keys_words, keys_scales, size, qs,
             ALU.mult,
         )
 
-        sized = [keep.tile([P, P, PACK], F32, name=f"sized{half}") for half in (0, 1)]
-        for half in (1, 0):
+        sized = [keep.tile([P, P, PACK], F32, name=f"sized{half}", tag=f"sized{half}") for half in (0, 1)]
+        for half in range(2):
             nc.vector.tensor_tensor(
                 sized[half][:],
                 gates[half][:],
                 vec_bank[:, P + half * P : P + (half + 1) * P].unsqueeze(2).to_broadcast([P, P, PACK]),
                 ALU.mult,
             )
-        weights = [keep.tile([P, G // 2, SPAN, PACK], BF16, name=f"weights{half}", align_bytes=64) for half in (0, 1)]
+        weights = [keep.tile([P, G // 2, SPAN, PACK], BF16, name=f"weights{half}", tag=f"weights{half}", align_bytes=64) for half in (0, 1)]
         for half in range(2):
             nc.vector.tensor_tensor(
                 weights[half][:],
@@ -177,6 +175,20 @@ def tile_attend_bspanread_v_kernel(tc, query, keys_words, keys_scales, size, qs,
                 in_=weights[half][:].rearrange("p g m r -> p (g m r)"),
             )
 
+        fade_turned = ps_back.tile([P, BANK], F32, name="fade_turned", tag="back")
+        nc.tensor.transpose(fade_turned[:, 0:P], rows[:], ident[:])
+        vec_cols = keep.tile([P, T_CHUNKS], F32, name="vec_cols", tag="dealt1", align_bytes=64)
+        nc.vector.tensor_copy(vec_cols[:], fade_turned[:, 0:T_CHUNKS])
+        per_bank = BANK // P
+        fade_banks = []
+        fade_rows = []
+        for b in range(T // BANK):
+            fade_bank = ps_turn.tile([P, BANK], F32, name="fade_bank")
+            for k in range(per_bank):
+                c = b * per_bank + k
+                nc.tensor.transpose(fade_bank[:, k * P : (k + 1) * P], vec_cols[:, c : c + 1].to_broadcast([P, P]), ident[:])
+            fade_banks.append(fade_bank)
+
         grows_lo = keep.tile([P, E // 2, PACK], BF16, name="grows_lo", align_bytes=64)
         grows_hi = keep.tile([P, E // 2, PACK], BF16, name="grows_hi", tag="after_exp", align_bytes=64)
         for j in range(2):
@@ -188,6 +200,10 @@ def tile_attend_bspanread_v_kernel(tc, query, keys_words, keys_scales, size, qs,
             grows_hi[:].rearrange("p (c i) r -> p c r i", i=4),
             grows_raw[:, :, E // 2 : E].rearrange("p r (c i) -> p c r i", i=4),
         )
+        for b in range(T // BANK):
+            fade_row = keep.tile([P, BANK], F32, name=f"fade_row{b}", tag=("after_exp2", "fade_row1")[b], align_bytes=64)
+            nc.scalar.copy(fade_row[:], fade_banks[b][:])
+            fade_rows.append(fade_row)
         grows_codes = [keep.tile([P, P], U32, name=f"grows_codes{j}", align_bytes=64) for j in range(E_TILES)]
         grows_scales = [keep.tile([P, P], U8, name=f"grows_scales{j}", align_bytes=64) for j in range(E_TILES)]
         for j in range(E_TILES):
@@ -201,7 +217,7 @@ def tile_attend_bspanread_v_kernel(tc, query, keys_words, keys_scales, size, qs,
         placed = []
         for j in range(E_TILES):
             window = keep.tile([P, T], F32, name=f"placed{j}")
-            nc.vector.memset(window[:].bitcast(I32), 0)
+            (nc.vector if j < 2 else nc.gpsimd).memset(window[:].bitcast(I32), 0)
             bank = ps_mm.tile([P, I], F32, name=f"grad_bank{j}", tag="mm")
             nc.tensor.matmul_mx(
                 out=bank[:],
@@ -217,11 +233,23 @@ def tile_attend_bspanread_v_kernel(tc, query, keys_words, keys_scales, size, qs,
             nc.vector.tensor_copy(window[:].indirect(offsets[:]), grads[:])
             placed.append(window)
 
-        per_bank = BANK // P
-        for j in range(E_TILES):
+        faded = {}
+        for b in range(T // BANK):
+            cols = slice(b * BANK, (b + 1) * BANK)
+            faded[0, b] = keep.tile([P, BANK], F32, name=f"faded0_{b}", tag=f"weights{b}", align_bytes=64)
+            nc.gpsimd.tensor_tensor(faded[0, b][:], old_tiles[0][:, cols], fade_rows[b][:], ALU.mult)
+            faded[1, b] = keep.tile([P, BANK], F32, name=f"faded1_{b}", tag=f"sized{b}")
+            nc.vector.tensor_tensor(faded[1, b][:], old_tiles[1][:, cols], fade_banks[b][:], ALU.mult)
+        for j in range(GPSIMD_TILES):
+            for b in range(T // BANK):
+                cols = slice(b * BANK, (b + 1) * BANK)
+                result = keep.tile([P, BANK], F32, name=f"result{j}_{b}")
+                nc.gpsimd.tensor_tensor(result[:], faded[j, b][:], placed[j][:, cols], ALU.add)
+                nc.sync.dma_start(out[j * P : (j + 1) * P, cols], result[:])
+        for j in range(GPSIMD_TILES, E_TILES):
             faded_t = keep.tile([P, T_CHUNKS, P], F32, name=f"faded_t{j}")
             for b in range(T // BANK):
-                turned = ps_turn.tile([P, per_bank, P], F32, name="turned")
+                turned = ps_mm.tile([P, per_bank, P], F32, name="turned", tag="mm")
                 for k in range(per_bank):
                     c = b * per_bank + k
                     nc.tensor.transpose(turned[:, k, :], old_tiles[j][:, c * P : (c + 1) * P], ident[:])
@@ -230,14 +258,9 @@ def tile_attend_bspanread_v_kernel(tc, query, keys_words, keys_scales, size, qs,
                     nc.scalar.activation(faded_t[:, c, :], turned[:, k, :], ACT.Copy, scale=vec_cols[:, c : c + 1])
             for b in range(T // BANK):
                 cols = slice(b * BANK, (b + 1) * BANK)
-                back = ps_back.tile([P, BANK], F32, name="back")
+                back = ps_back.tile([P, BANK], F32, name="back", tag="back")
                 for k in range(per_bank):
                     nc.tensor.transpose(back[:, k * P : (k + 1) * P], faded_t[:, b * per_bank + k, :], ident[:])
                 result = keep.tile([P, BANK], F32, name=f"result{j}_{b}")
-                if j < GPSIMD_TILES:
-                    faded = keep.tile([P, BANK], F32, name=f"faded{j}_{b}")
-                    nc.scalar.copy(faded[:], back[:])
-                    nc.gpsimd.tensor_tensor(result[:], faded[:], placed[j][:, cols], ALU.add)
-                else:
-                    nc.vector.tensor_tensor(result[:], back[:], placed[j][:, cols], ALU.add)
+                nc.vector.tensor_tensor(result[:], back[:], placed[j][:, cols], ALU.add)
                 nc.sync.dma_start(out[j * P : (j + 1) * P, cols], result[:])

from contextlib import ExitStack

import concourse.mybir as mybir
from concourse.masks import make_identity

D, E, T, I, Q, G = 512, 512, 1024, 256, 512, 32
FLOPS = 2 * D * Q * I + 2 * Q * E * I

F32 = mybir.dt.float32
BF16 = mybir.dt.bfloat16
I32 = mybir.dt.int32
U32 = mybir.dt.uint32
U16 = mybir.dt.uint16
U8 = mybir.dt.uint8
FP8X4 = mybir.dt.float8_e4m3fn_x4
FP4X4 = mybir.dt.float4_e2m1fn_x4
ALU = mybir.AluOpType
ACT = mybir.ActivationFunctionType
AXIS_X = mybir.AxisListType.X

P = 128
PACK = 4
SPAN = I // G
E_TILES = E // P
T_CHUNKS = T // P
BANK = 512
GPSIMD_TILES = 2


def tile_attend_bspanread_v_kernel(tc, query, keys_words, keys_scales, size, qs, grows, old, fade, offs, out):
    nc = tc.nc
    with ExitStack() as ctx:
        keep = ctx.enter_context(tc.tile_pool(name="keep", bufs=1))
        ps_mm = ctx.enter_context(tc.psum_pool(name="ps_mm", bufs=2))
        ps_vec = ctx.enter_context(tc.psum_pool(name="ps_vec", bufs=1))
        ps_turn = ctx.enter_context(tc.psum_pool(name="ps_turn", bufs=2))
        ps_back = ctx.enter_context(tc.psum_pool(name="ps_back", bufs=3))

        offsets = keep.tile([P, I // 16], U16, name="offsets")
        nc.sync.dma_start(offsets[:], offs)
        pool_scales = keep.tile([P, T], U8, name="pool_scales", tag="then_old0", align_bytes=64)
        nc.gpsimd.memset(pool_scales[:].bitcast(I32), 0)
        rows = keep.tile([P, P], F32, name="rows")
        nc.gpsimd.memset(rows[:], 0.0)
        pool_words = keep.tile([P, T], U16, name="pool_words", tag="then_grows")
        nc.sync.dma_start(pool_words[:].bitcast(I32), keys_words[0].bitcast(I32))
        for quad in range(4):
            nc.scalar.dma_start(
                pool_scales[32 * quad : 32 * quad + 4, :].bitcast(I32),
                keys_scales[0, 4 * quad : 4 * quad + 4, :].bitcast(I32),
            )
        query_rows = query.rearrange("(p j) q -> p j q", j=PACK)
        query_raw = []
        for half in range(2):
            raw = keep.tile([P, PACK, Q // 2], F32, name=f"query_raw{half}", tag=f"then_old{half + 1}", align_bytes=64)
            nc.sync.dma_start(raw[:], query_rows[:, :, half * (Q // 2) : (half + 1) * (Q // 2)])
            query_raw.append(raw)
        qs_cols = keep.tile([P, PACK], F32, name="qs_cols")
        nc.sync.dma_start(qs_cols[:], qs.rearrange("(s r) one -> s (r one)", r=PACK))
        nc.sync.dma_start(rows[0:T_CHUNKS, :], fade.rearrange("one (c p) -> (one c) p", p=P))
        size_cols = keep.tile([P, 2], F32, name="size_cols")
        with nc.allow_non_contiguous_dma(reason="one value of size to a partition"):
            nc.scalar.dma_start(size_cols[:], size.rearrange("one (h p) -> p (one h)", p=P))

        ident = keep.tile([P, P], F32, name="ident")
        make_identity(nc, ident[:])

        key_words = keep.tile([P, I], U16, name="key_words", align_bytes=64)
        key_scales = keep.tile([P, I], U8, name="key_scales", align_bytes=64)
        nc.vector.tensor_copy(key_words[:], pool_words[:].indirect(offsets[:]))
        nc.vector.tensor_copy(key_scales[:], pool_scales[:].indirect(offsets[:]))

        query_codes = [keep.tile([P, P], U32, name=f"query_codes{r}", align_bytes=64) for r in range(PACK)]
        query_scales = [keep.tile([P, P], U8, name=f"query_scales{r}", align_bytes=64) for r in range(PACK)]
        for half in range(2):
            dealt = keep.tile([P, PACK, P // 2, PACK], BF16, name=f"query_dealt{half}", tag=("then_old3", "dealt1")[half], align_bytes=64)
            nc.vector.tensor_copy(
                dealt[:].rearrange("p r s j -> p s r j"),
                query_raw[half][:].rearrange("p j (s r) -> p s r j", r=PACK),
            )
            cols = slice(half * (P // 2), (half + 1) * (P // 2))
            for r in range(PACK):
                nc.vector.quantize_mx(
                    out=query_codes[r][:, cols].bitcast(FP8X4),
                    scales=query_scales[r][:, cols],
                    in_=dealt[:, r].rearrange("p s j -> p (s j)"),
                )

        grows_raw = keep.tile([P, PACK, E], F32, name="grows_raw", tag="then_grows")
        nc.sync.dma_start(grows_raw[:], grows.rearrange("(s r) e -> s r e", r=PACK))
        old_tiles = []
        for j in range(E_TILES):
            old_tile = keep.tile([P, T], F32, name=f"old{j}", tag=f"then_old{j}", align_bytes=64)
            nc.sync.dma_start(old_tile[:], old[j * P : (j + 1) * P, :])
            old_tiles.append(old_tile)

        vec_bank = ps_vec.tile([P, P + I], F32, name="vec_bank")
        for half in range(2):
            nc.tensor.transpose(
                vec_bank[:, P + half * P : P + (half + 1) * P],
                size_cols[:, half : half + 1].to_broadcast([P, P]),
                ident[:],
            )

        score_banks = []
        for half in range(2):
            score_banks.append(ps_mm.tile([P, PACK, P], F32, name=f"scores{half}", tag="mm"))
        for half in range(2):
            for r in range(PACK):
                slots = slice(half * P, (half + 1) * P)
                nc.tensor.matmul_mx(
                    out=score_banks[half][:, r, :],
                    lhsT=query_codes[r][:].bitcast(FP8X4),
                    lhsT_scale=query_scales[r][:],
                    rhs=key_words[:, slots].bitcast(FP4X4),
                    rhs_scale=key_scales[:, slots],
                    start=True,
                    stop=True,
                )

        span_sums = keep.tile([P, PACK, G], F32, name="span_sums")
        gates = [keep.tile([P, P, PACK], F32, name=f"gates{half}") for half in range(2)]
        for half in range(2):
            nc.scalar.activation(gates[half][:], score_banks[half][:].rearrange("p r i -> p i r"), ACT.Sigmoid)
            nc.vector.tensor_reduce(
                out=span_sums[:, :, half * (G // 2) : (half + 1) * (G // 2)],
                in_=score_banks[half][:].rearrange("p r (g m) -> p r g m", m=SPAN),
                axis=AXIS_X,
                op=ALU.add,
            )

        neg_max = keep.tile([P, PACK], F32, name="neg_max")
        nc.vector.tensor_reduce(out=neg_max[:], in_=span_sums[:], axis=AXIS_X, op=ALU.max, negate=True)
        shifted = keep.tile([P, PACK, G], F32, name="shifted", tag="after_exp", align_bytes=64)
        nc.vector.tensor_tensor(shifted[:], span_sums[:], neg_max[:].unsqueeze(2).to_broadcast([P, PACK, G]), ALU.add)
        probs = keep.tile([P, PACK, G], F32, name="probs", tag="after_exp2", align_bytes=64)
        nc.scalar.activation(probs[:], shifted[:], ACT.Exp, scale=1.0 / SPAN)
        row_sums = keep.tile([P, PACK], F32, name="row_sums")
        nc.vector.tensor_reduce(out=row_sums[:], in_=probs[:], axis=AXIS_X, op=ALU.add)
        probs_qs = keep.tile([P, PACK, G], F32, name="probs_qs", tag="fade_row1", align_bytes=64)
        nc.vector.tensor_tensor(probs_qs[:], probs[:], qs_cols[:].unsqueeze(2).to_broadcast([P, PACK, G]), ALU.mult)
        inv_sums = keep.tile([P, PACK], F32, name="inv_sums")
        nc.vector.reciprocal(inv_sums[:], row_sums[:])
        shares = keep.tile([P, G, PACK], F32, name="shares")
        nc.vector.tensor_tensor(
            shares[:],
            probs_qs[:].rearrange("p r g -> p g r"),
            inv_sums[:].unsqueeze(1).to_broadcast([P, G, PACK]),
            ALU.mult,
        )

        sized = [keep.tile([P, P, PACK], F32, name=f"sized{half}", tag=f"sized{half}") for half in (0, 1)]
        for half in range(2):
            nc.vector.tensor_tensor(
                sized[half][:],
                gates[half][:],
                vec_bank[:, P + half * P : P + (half + 1) * P].unsqueeze(2).to_broadcast([P, P, PACK]),
                ALU.mult,
            )
        weights = [keep.tile([P, G // 2, SPAN, PACK], BF16, name=f"weights{half}", tag=f"weights{half}", align_bytes=64) for half in (0, 1)]
        for half in range(2):
            nc.vector.tensor_tensor(
                weights[half][:],
                sized[half][:].rearrange("p (g m) r -> p g m r", m=SPAN),
                shares[:, half * (G // 2) : (half + 1) * (G // 2), :].unsqueeze(2).to_broadcast([P, G // 2, SPAN, PACK]),
                ALU.mult,
            )
        weight_codes = keep.tile([P, I], U32, name="weight_codes", align_bytes=64)
        weight_scales = keep.tile([P, I], U8, name="weight_scales", align_bytes=64)
        for half in range(2):
            slots = slice(half * P, (half + 1) * P)
            nc.vector.quantize_mx(
                out=weight_codes[:, slots].bitcast(FP8X4),
                scales=weight_scales[:, slots],
                in_=weights[half][:].rearrange("p g m r -> p (g m r)"),
            )

        fade_turned = ps_back.tile([P, BANK], F32, name="fade_turned", tag="back")
        nc.tensor.transpose(fade_turned[:, 0:P], rows[:], ident[:])
        vec_cols = keep.tile([P, T_CHUNKS], F32, name="vec_cols", tag="dealt1", align_bytes=64)
        nc.vector.tensor_copy(vec_cols[:], fade_turned[:, 0:T_CHUNKS])
        per_bank = BANK // P
        fade_banks = []
        fade_rows = []
        for b in range(T // BANK):
            fade_bank = ps_turn.tile([P, BANK], F32, name="fade_bank")
            for k in range(per_bank):
                c = b * per_bank + k
                nc.tensor.transpose(fade_bank[:, k * P : (k + 1) * P], vec_cols[:, c : c + 1].to_broadcast([P, P]), ident[:])
            fade_banks.append(fade_bank)

        grows_lo = keep.tile([P, E // 2, PACK], BF16, name="grows_lo", align_bytes=64)
        grows_hi = keep.tile([P, E // 2, PACK], BF16, name="grows_hi", tag="after_exp", align_bytes=64)
        for j in range(2):
            nc.vector.tensor_copy(
                grows_lo[:, j * P : (j + 1) * P, :].rearrange("p (c i) r -> p c r i", i=4),
                grows_raw[:, :, j * P : (j + 1) * P].rearrange("p r (c i) -> p c r i", i=4),
            )
        nc.scalar.copy(
            grows_hi[:].rearrange("p (c i) r -> p c r i", i=4),
            grows_raw[:, :, E // 2 : E].rearrange("p r (c i) -> p c r i", i=4),
        )
        for b in range(T // BANK):
            fade_row = keep.tile([P, BANK], F32, name=f"fade_row{b}", tag=("after_exp2", "fade_row1")[b], align_bytes=64)
            nc.scalar.copy(fade_row[:], fade_banks[b][:])
            fade_rows.append(fade_row)
        grows_codes = [keep.tile([P, P], U32, name=f"grows_codes{j}", align_bytes=64) for j in range(E_TILES)]
        grows_scales = [keep.tile([P, P], U8, name=f"grows_scales{j}", align_bytes=64) for j in range(E_TILES)]
        for j in range(E_TILES):
            woven = grows_lo if j < 2 else grows_hi
            nc.vector.quantize_mx(
                out=grows_codes[j][:].bitcast(FP8X4),
                scales=grows_scales[j][:],
                in_=woven[:, (j % 2) * P : (j % 2 + 1) * P, :].rearrange("p e r -> p (e r)"),
            )

        placed = []
        for j in range(E_TILES):
            window = keep.tile([P, T], F32, name=f"placed{j}")
            (nc.vector if j < 2 else nc.gpsimd).memset(window[:].bitcast(I32), 0)
            bank = ps_mm.tile([P, I], F32, name=f"grad_bank{j}", tag="mm")
            nc.tensor.matmul_mx(
                out=bank[:],
                lhsT=grows_codes[j][:].bitcast(FP8X4),
                lhsT_scale=grows_scales[j][:],
                rhs=weight_codes[:].bitcast(FP8X4),
                rhs_scale=weight_scales[:],
                start=True,
                stop=True,
            )
            grads = keep.tile([P, I], F32, name=f"grads{j}")
            nc.scalar.copy(grads[:], bank[:])
            nc.vector.tensor_copy(window[:].indirect(offsets[:]), grads[:])
            placed.append(window)

        faded = {}
        for b in range(T // BANK):
            cols = slice(b * BANK, (b + 1) * BANK)
            faded[0, b] = keep.tile([P, BANK], F32, name=f"faded0_{b}", tag=f"weights{b}", align_bytes=64)
            nc.gpsimd.tensor_tensor(faded[0, b][:], old_tiles[0][:, cols], fade_rows[b][:], ALU.mult)
            faded[1, b] = keep.tile([P, BANK], F32, name=f"faded1_{b}", tag=f"sized{b}")
            nc.vector.tensor_tensor(faded[1, b][:], old_tiles[1][:, cols], fade_banks[b][:], ALU.mult)
        for j in range(GPSIMD_TILES):
            for b in range(T // BANK):
                cols = slice(b * BANK, (b + 1) * BANK)
                result = keep.tile([P, BANK], F32, name=f"result{j}_{b}")
                nc.gpsimd.tensor_tensor(result[:], faded[j, b][:], placed[j][:, cols], ALU.add)
                nc.sync.dma_start(out[j * P : (j + 1) * P, cols], result[:])
        for j in range(GPSIMD_TILES, E_TILES):
            faded_t = keep.tile([P, T_CHUNKS, P], F32, name=f"faded_t{j}")
            for b in range(T // BANK):
                turned = ps_mm.tile([P, per_bank, P], F32, name="turned", tag="mm")
                for k in range(per_bank):
                    c = b * per_bank + k
                    nc.tensor.transpose(turned[:, k, :], old_tiles[j][:, c * P : (c + 1) * P], ident[:])
                for k in range(per_bank):
                    c = b * per_bank + k
                    nc.scalar.activation(faded_t[:, c, :], turned[:, k, :], ACT.Copy, scale=vec_cols[:, c : c + 1])
            for b in range(T // BANK):
                cols = slice(b * BANK, (b + 1) * BANK)
                back = ps_back.tile([P, BANK], F32, name="back", tag="back")
                for k in range(per_bank):
                    nc.tensor.transpose(back[:, k * P : (k + 1) * P], faded_t[:, b * per_bank + k, :], ident[:])
                result = keep.tile([P, BANK], F32, name=f"result{j}_{b}")
                nc.vector.tensor_tensor(result[:], back[:], placed[j][:, cols], ALU.add)
                nc.sync.dma_start(out[j * P : (j + 1) * P, cols], result[:])
